import numpy as np
import ml_dtypes


def mxq(x, axis, fmt="e4m3"):
    dtype, down = {"e4m3": (ml_dtypes.float8_e4m3fn, 7), "e5m2": (ml_dtypes.float8_e5m2, 14)}[fmt]
    v = np.moveaxis(np.asarray(x, np.float32).astype(ml_dtypes.bfloat16).astype(np.float64), axis, -1)
    blocks = v.reshape(v.shape[:-1] + (-1, 32))
    amax = np.abs(blocks).max(-1, keepdims=True)
    byte = np.maximum(np.where(amax > 0, np.frexp(amax)[1] - 1 + 127, 0) - down, 1)
    scale = np.exp2(byte - 127.0)
    codes = (blocks / scale).astype(np.float32).astype(dtype).astype(np.float64)
    return np.moveaxis((codes * scale).reshape(v.shape), -1, axis)


WIDE = False


def mx_kscale(k):
    if not WIDE:
        return np.ones(k)
    levels = np.array([18, -18])
    if k % 512:
        return np.exp2(np.random.permutation(np.resize(levels, k // 32))).repeat(32)
    a = np.empty((k // 512, 16))
    for p in range(k // 512):
        a[p, :8] = np.random.permutation(np.resize(levels, 8))
        for g in range(8):
            far = levels[np.abs(levels - a[p, g]) >= 10]
            a[p, g + 8] = far[np.random.randint(len(far))]
    return np.exp2(a.ravel()).repeat(32)


def f64(x):
    return np.asarray(x).astype(np.float64)


def striped(idx):
    return np.tile(np.asarray(idx).reshape(-1, 16).T, (8, 1)).astype(np.uint16)


def unstriped(offs):
    return offs[:16].T.reshape(-1).astype(np.int64)

def planes(y):
    n, m = y.shape
    v = y.astype(np.float32).astype(ml_dtypes.bfloat16).astype(np.float64).reshape(n // 32, 32, m)
    top = np.abs(v).max(1)
    byte = np.clip(np.where(top > 0, np.frexp(top)[1] - 1 + 127 - 7, 1), 1, 254)
    codes = (v * np.exp2(127.0 - byte)[:, None, :]).reshape(n, m).astype(np.float32).astype(ml_dtypes.float8_e4m3fn).view(np.uint8)
    words = codes.reshape(n // 512, 128, 4, m).transpose(0, 1, 3, 2)
    return np.ascontiguousarray(words), np.ascontiguousarray(byte.astype(np.uint8).reshape(n // 512, 16, m))


def setup_inputs():
    n = np.random.standard_normal
    uni = np.random.uniform
    idx = np.random.permutation(2048)[:512]
    f_e = mx_kscale(512)
    f_i = np.ones(2048)
    f_i[idx] = mx_kscale(512)
    return {
        "aT": (n((512, 2048)) / np.sqrt(512) * f_i[None, :]).astype(np.float32),
        "bT": (n((512, 2048)) * f_e[:, None] / f_i[None, :]).astype(np.float32),
        "tg": (n((512, 512))).astype(np.float32),
        "wm": (uni(0.75, 1.3, (512, 512))).astype(np.float32),
        "ca": (uni(0.75, 1.3, (512, 1))).astype(np.float32),
        "cb": np.tile(uni(0.75, 1.3, 512) / f_e, (128, 1)).astype(np.float32),
        "offs": striped(idx),
    }


def reference(aT, bT, tg, wm, ca, cb, offs):
    idx = unstriped(offs)
    aT_i = f64(aT)[:, idx]
    bT_i = f64(bT)[:, idx]
    C = mxq(aT_i, 1, "e4m3") @ mxq(bT_i, 1, "e4m3").T
    M = f64(wm) * f64(ca) * f64(cb)[:1] * (f64(ca) * f64(cb)[:1] * C - f64(tg))
    da = mxq(M, 1, "e5m2") @ mxq(bT_i, 0, "e4m3")
    out_0 = np.zeros((512, 2048))
    out_0[:, idx] = da
    return (out_0,) + planes(out_0)

@@ -1,0 +1,278 @@
+from contextlib import ExitStack
+
+import concourse.mybir as mybir
+from concourse.masks import make_identity
+
+D, E, N, T = 512, 512, 512, 2048
+FLOPS = 2 * 2 * D * E * N
+
+F32 = mybir.dt.float32
+BF16 = mybir.dt.bfloat16
+I32 = mybir.dt.int32
+U32 = mybir.dt.uint32
+U16 = mybir.dt.uint16
+U8 = mybir.dt.uint8
+E4M3 = mybir.dt.float8_e4m3fn_x4
+E5M2 = mybir.dt.float8_e5m2_x4
+MULT = mybir.AluOpType.mult
+COPY = mybir.ActivationFunctionType.Copy
+
+P = 128
+PACK = 4
+CHUNK = 512
+HALF = T // 2
+ALIGN = 64
+
+
+def tile_attend_gbarlow_a_pl_kernel(tc, aT, bT, tg, wm, ca, cb, offs, out_0, out_1, out_2):
+    nc = tc.nc
+    lanes = [(k + 1) % PACK for k in range(PACK)]
+    a_rows = aT.rearrange("(p j) c -> j p c", j=PACK)
+    b_rows = bT.rearrange("(p t) c -> t p c", t=PACK)
+    tg_rows = tg.rearrange("(p j) e -> j p e", j=PACK)
+    wm_rows = wm.rearrange("(p j) e -> j p e", j=PACK)
+    out_rows = out_0.rearrange("(p j) c -> j p c", j=PACK)
+    out_words = out_1[0].rearrange("p c l -> p (c l)").bitcast(I32)
+    out_scales = out_2[0].bitcast(I32)
+
+    with ExitStack() as ctx:
+        keep = ctx.enter_context(tc.tile_pool(name="keep", bufs=1))
+        psum1 = ctx.enter_context(tc.psum_pool(name="psum1", bufs=1))
+        psum2 = ctx.enter_context(tc.psum_pool(name="psum2", bufs=2))
+
+        def sbuf(shape, dtype, name, reuses=None):
+            return keep.tile(shape, dtype, name=name, tag=reuses or name, align_bytes=ALIGN)
+
+        offsets = keep.tile([P, N // 16], U16, name="offsets")
+        nc.sync.dma_start(offsets[:], offs)
+        cb_col = sbuf([P, PACK], F32, "cb_col")
+        nc.scalar.dma_start(cb_col[:], cb[0].rearrange("(p t) -> p t", t=PACK))
+        ca_col = sbuf([P, PACK], F32, "ca_col")
+        nc.scalar.dma_start(ca_col[:], ca.rearrange("(p j) o -> p (j o)", j=PACK))
+
+        b_win = [sbuf([P, T], F32, f"b_win{t}") for t in range(PACK)]
+        a_win = [sbuf([P, T], F32, f"a_win{k}") for k in range(PACK)]
+        tg_sb = [sbuf([P, E], F32, f"tg_sb{k}") for k in range(PACK)]
+        wm_sb = [sbuf([P, E], F32, f"wm_sb{k}") for k in range(PACK)]
+        for t in range(PACK):
+            nc.sync.dma_start(b_win[t][:], b_rows[t])
+        for k in range(PACK):
+            if k < PACK - 1:
+                nc.sync.dma_start(a_win[k][:], a_rows[lanes[k]])
+            nc.sync.dma_start(wm_sb[k][:], wm_rows[lanes[k]])
+            nc.sync.dma_start(tg_sb[k][:], tg_rows[lanes[k]])
+        nc.sync.dma_start(a_win[PACK - 1][:], a_rows[lanes[PACK - 1]])
+
+        ident = sbuf([P, P], F32, "ident")
+        make_identity(nc, ident[:])
+
+        neg_cb_col = sbuf([P, PACK], F32, "neg_cb_col")
+        nc.scalar.activation(neg_cb_col[:], cb_col[:], COPY, scale=-1.0)
+        spread = psum1.tile([P, PACK, P], F32, name="spread", tag="w_bank")
+        for t in range(PACK):
+            nc.tensor.transpose(spread[:, t, :], neg_cb_col[:, t : t + 1].to_broadcast([P, P]), ident[:])
+        neg_cb_row = sbuf([P, E], F32, "neg_cb_row")
+        nc.scalar.copy(neg_cb_row[:], spread[:].rearrange("p t q -> p (t q)"))
+
+        def zeroed_window(k):
+            window = sbuf([P, T], F32, f"out_win{k}")
+            (nc.vector if k < 2 else nc.gpsimd).memset(window[:], 0.0)
+            return window
+
+        def gather(window, name):
+            picked = sbuf([P, N], BF16, name)
+            nc.vector.tensor_copy(picked[:], window[:].indirect(offsets[:]))
+            return picked
+
+        def turn_slots(picked):
+            words = picked[:].bitcast(F32)
+            turned = psum2.tile([P, 2, P], F32, name="turned")
+            for u in range(2):
+                nc.tensor.transpose(turned[:, u, :], words[:, u : N // 2 : 2], ident[:])
+            return turned
+
+        def group_slots(turned, grouped):
+            nc.scalar.copy(
+                grouped.bitcast(F32).rearrange("p (q u) -> p q u", u=2), turned[:].rearrange("p u q -> p q u")
+            )
+
+        out_win = [zeroed_window(k) for k in range(PACK)]
+        b_grouped = sbuf([P, 2 * N * PACK], BF16, "b_grouped")
+        be_grouped = b_grouped[:, N * PACK :].rearrange("p (i t) -> p i t", t=PACK)
+        for t in range(PACK):
+            picked = gather(b_win[t], f"b_picked{t}")
+            group_slots(turn_slots(picked), b_grouped[:, t * N : (t + 1) * N])
+            if t < 2:
+                nc.scalar.copy(be_grouped[:, :, t], picked[:])
+            else:
+                nc.vector.tensor_copy(be_grouped[:, :, t], picked[:])
+
+        a_picked = [gather(a_win[k], f"a_picked{k}") for k in range(PACK)]
+
+        b_codes = sbuf([P, E + N], U32, "b_codes", "a_win0")
+        b_scales = sbuf([P, E + N], U8, "b_scales")
+        nc.vector.quantize_mx(out=b_codes[:].bitcast(E4M3), scales=b_scales[:], in_=b_grouped[:])
+
+        after_a1 = sbuf([P, N], BF16, "after_a1", "a_win1")
+        after_a2 = sbuf([P, 5 * N], F32, "after_a2", "a_win2")
+        after_a3 = sbuf([P, 2 * N], F32, "after_a3", "a_win3")
+        a_grouped = [
+            after_a3[:, N // 2 : N].bitcast(BF16) if k == 2 else sbuf([P, N], BF16, f"a_grouped{k}")[:]
+            for k in range(PACK)
+        ]
+        m_grouped = [after_a1[:], after_a3[:, : N // 2].bitcast(BF16)]
+        m_grouped += [sbuf([P, N], BF16, f"m_grouped{k}")[:] for k in (2, 3)]
+        scaled = [after_a2[:, :N] if k == 1 else sbuf([P, E], F32, f"scaled{k}")[:] for k in range(PACK)]
+        weight = [
+            sbuf([P, E], F32, "weight0")[:],
+            after_a2[:, 2 * N : 3 * N],
+            sbuf([P, E], F32, "weight2")[:],
+            after_a3[:, N:],
+        ]
+
+        def correlate(k):
+            group_slots(turn_slots(a_picked[k]), a_grouped[k])
+            a_codes = sbuf([P, P], U32, f"a_codes{k}")
+            a_scales = sbuf([P, P], U8, f"a_scales{k}")
+            nc.vector.quantize_mx(out=a_codes[:].bitcast(E4M3), scales=a_scales[:], in_=a_grouped[k])
+            corr = psum2.tile([P, E], F32, name="corr")
+            nc.tensor.matmul_mx(
+                out=corr[:],
+                lhsT=a_codes[:].bitcast(E4M3),
+                lhsT_scale=a_scales[:],
+                rhs=b_codes[:, :E].bitcast(E4M3),
+                rhs_scale=b_scales[:, :E],
+                start=True,
+                stop=True,
+            )
+            ca_k = ca_col[:, lanes[k] : lanes[k] + 1]
+            nc.vector.scalar_tensor_tensor(scaled[k], corr[:], ca_k, neg_cb_row[:], MULT, MULT)
+
+        def deal(k, dealt):
+            ca_k = ca_col[:, lanes[k] : lanes[k] + 1]
+            nc.scalar.activation(
+                dealt[:, :E].rearrange("p (t q) -> p q t", t=PACK),
+                wm_sb[k][:].rearrange("p (q t) -> p q t", t=PACK),
+                COPY,
+                scale=ca_k,
+            )
+            nc.scalar.copy(
+                dealt[:, E:].rearrange("p (t q) -> p q t", t=PACK), tg_sb[k][:].rearrange("p (q t) -> p q t", t=PACK)
+            )
+            return dealt
+
+        def make_weight(k, dealt):
+            w_bank = psum1.tile([P, PACK, P], F32, name="w_bank", tag="w_bank")
+            for t in range(PACK):
+                nc.tensor.transpose(w_bank[:, t, :], dealt[:, t * P : (t + 1) * P], ident[:])
+            for t in range(PACK):
+                nc.scalar.activation(
+                    weight[k][:, t * P : (t + 1) * P], w_bank[:, t, :], COPY, scale=neg_cb_col[:, t : t + 1]
+                )
+
+        def make_m(k, dealt):
+            resid = psum2.tile([P, PACK, P], F32, name="resid")
+            for t in range(PACK):
+                nc.tensor.matmul(
+                    resid[:, t, :],
+                    dealt[:, E + t * P : E + (t + 1) * P],
+                    ident[:],
+                    is_transpose=True,
+                    start=(t == 0),
+                    stop=False,
+                )
+            for t in range(PACK):
+                nc.tensor.matmul(
+                    resid[:, t, :],
+                    scaled[k][:, t * P : (t + 1) * P],
+                    ident[:],
+                    is_transpose=True,
+                    start=False,
+                    stop=(t == PACK - 1),
+                )
+            nc.vector.tensor_tensor(
+                m_grouped[k].rearrange("p (c i t) -> p c t i", i=4, t=PACK),
+                resid[:].rearrange("p t (c i) -> p c t i", i=4),
+                weight[k].rearrange("p (t c i) -> p c t i", i=4, t=PACK),
+                MULT,
+            )
+            m_codes = sbuf([P, P], U32, f"m_codes{k}")
+            m_scales = sbuf([P, P], U8, f"m_scales{k}")
+            nc.vector.quantize_mx(out=m_codes[:].bitcast(E5M2), scales=m_scales[:], in_=m_grouped[k])
+            return m_codes, m_scales
+
+        def place_gradient(k, m_codes, m_scales):
+            if k == 2:
+                grad = psum2.tile([P, N], F32, name="grad2", tag="turned")
+            else:
+                grad = psum1.tile([P, N], F32, name=f"grad{k}", tag="w_bank" if k == 3 else "grad")
+            nc.tensor.matmul_mx(
+                out=grad[:],
+                lhsT=m_codes[:].bitcast(E5M2),
+                lhsT_scale=m_scales[:],
+                rhs=b_codes[:, E:].bitcast(E4M3),
+                rhs_scale=b_scales[:, E:],
+                start=True,
+                stop=True,
+            )
+            if k == 0:
+                grad_sb = after_a2[:, N : 2 * N]
+            else:
+                grad_sb = sbuf([P, N], F32, f"grad_sb{k}", "scaled3" if k == 1 else None)[:]
+            nc.scalar.copy(grad_sb, grad[:])
+            nc.vector.tensor_copy(out_win[k][:].indirect(offsets[:]), grad_sb)
+            nc.sync.dma_start(out_rows[lanes[k]], out_win[k][:])
+
+        correlate(0)
+        dealt0 = deal(0, sbuf([P, 2 * E], F32, "dealt0", "a_picked0")[:])
+        make_weight(0, dealt0)
+        m0 = make_m(0, dealt0)
+        correlate(1)
+        dealt1 = deal(1, sbuf([P, 2 * E], F32, "dealt1", "a_picked1")[:])
+        place_gradient(0, *m0)
+        make_weight(1, dealt1)
+        dealt2 = deal(2, after_a2[:, 3 * N :])
+        make_weight(2, dealt2)
+        dealt3 = deal(3, sbuf([P, 2 * E], F32, "dealt3", "tg_sb2")[:])
+        m1 = make_m(1, dealt1)
+        correlate(2)
+        correlate(3)
+        make_weight(3, dealt3)
+        m2 = make_m(2, dealt2)
+        m3 = make_m(3, dealt3)
+        place_gradient(1, *m1)
+        place_gradient(2, *m2)
+        place_gradient(3, *m3)
+
+        pairs = [
+            sbuf([P, 2, HALF, 2], BF16, "pairs0", "a_picked3"),
+            sbuf([P, 2, HALF, 2], BF16, "pairs1", "a_grouped3"),
+        ]
+
+        def round_plane(engine_copy, k, half):
+            lane = lanes[k]
+            engine_copy(pairs[half][:, lane // 2, :, lane % 2], out_win[k][:, half * HALF : (half + 1) * HALF])
+
+        for k in range(PACK - 1):
+            for half in range(2):
+                round_plane(nc.scalar.copy, k, half)
+
+        plane_scales = sbuf([P, T], U8, "plane_scales")
+        copies = [nc.vector.tensor_copy, nc.scalar.copy]
+        laid = [sbuf([P, CHUNK * PACK], BF16, f"laid{c}") for c in range(T // CHUNK)]
+        for half in range(2):
+            round_plane(copies[half], PACK - 1, half)
+            words = pairs[half][:].rearrange("p u q h -> p u (q h)").bitcast(F32)
+            for part in range(2):
+                copies[half](
+                    laid[2 * half + part][:].bitcast(F32).rearrange("p (q u) -> p q u", u=2),
+                    words[:, :, part * CHUNK : (part + 1) * CHUNK].rearrange("p u q -> p q u"),
+                )
+        for c in range(T // CHUNK):
+            cols = slice(c * CHUNK, (c + 1) * CHUNK)
+            plane_codes = sbuf([P, CHUNK], U32, f"plane_codes{c}")
+            nc.vector.quantize_mx(out=plane_codes[:].bitcast(E4M3), scales=plane_scales[:, cols], in_=laid[c][:])
+            nc.sync.dma_start(out_words[:, cols], plane_codes[:].bitcast(I32))
+        for q in range(4):
+            queue = nc.sync if q % 2 == 0 else nc.scalar
+            queue.dma_start(out_scales[4 * q : 4 * q + 4, :], plane_scales[32 * q : 32 * q + 4, :].bitcast(I32))

@@ -54,14 +54,16 @@ def tile_attend_gbarlow_a_pl_kernel(tc, aT, bT, tg, wm, ca, cb, offs, out_0, out
         a_win = [sbuf([P, T], F32, f"a_win{k}") for k in range(PACK)]
         tg_sb = [sbuf([P, E], F32, f"tg_sb{k}") for k in range(PACK)]
         wm_sb = [sbuf([P, E], F32, f"wm_sb{k}") for k in range(PACK)]
-        for t in range(PACK):
+        for t in range(PACK - 1):
             nc.sync.dma_start(b_win[t][:], b_rows[t])
-        for k in range(PACK):
-            if k < PACK - 1:
+        nc.sync.dma_start(a_win[0][:], a_rows[lanes[0]])
+        nc.sync.dma_start(b_win[PACK - 1][:], b_rows[PACK - 1])
+        for windows, weighted in (((), (0,)), ((1,), (1,)), ((2, 3), (2, 3))):
+            for k in windows:
                 nc.sync.dma_start(a_win[k][:], a_rows[lanes[k]])
-            nc.sync.dma_start(wm_sb[k][:], wm_rows[lanes[k]])
-            nc.sync.dma_start(tg_sb[k][:], tg_rows[lanes[k]])
-        nc.sync.dma_start(a_win[PACK - 1][:], a_rows[lanes[PACK - 1]])
+            for k in weighted:
+                nc.sync.dma_start(wm_sb[k][:], wm_rows[lanes[k]])
+                nc.sync.dma_start(tg_sb[k][:], tg_rows[lanes[k]])
 
         ident = sbuf([P, P], F32, "ident")
         make_identity(nc, ident[:])
@@ -79,8 +81,8 @@ def tile_attend_gbarlow_a_pl_kernel(tc, aT, bT, tg, wm, ca, cb, offs, out_0, out
             (nc.vector if k < 2 else nc.gpsimd).memset(window[:], 0.0)
             return window
 
-        def gather(window, name):
-            picked = sbuf([P, N], BF16, name)
+        def gather(window, name, reuses=None):
+            picked = sbuf([P, N], BF16, name, reuses)
             nc.vector.tensor_copy(picked[:], window[:].indirect(offsets[:]))
             return picked
 
@@ -99,83 +101,77 @@ def tile_attend_gbarlow_a_pl_kernel(tc, aT, bT, tg, wm, ca, cb, offs, out_0, out
         out_win = [zeroed_window(k) for k in range(PACK)]
         b_grouped = sbuf([P, 2 * N * PACK], BF16, "b_grouped")
         be_grouped = b_grouped[:, N * PACK :].rearrange("p (i t) -> p i t", t=PACK)
+
+        def quantize_a(k, picked, grouped, reuses=None):
+            group_slots(turn_slots(picked), grouped)
+            a_codes = sbuf([P, P], U32, f"a_codes{k}", reuses)
+            a_scales = sbuf([P, P], U8, f"a_scales{k}")
+            nc.vector.quantize_mx(out=a_codes[:].bitcast(E4M3), scales=a_scales[:], in_=grouped)
+            return a_codes, a_scales
+
         for t in range(PACK):
+            if t == PACK - 1:
+                codes0 = quantize_a(0, gather(a_win[0], "a_picked0"), sbuf([P, N], BF16, "a_grouped0")[:], "b_win3")
             picked = gather(b_win[t], f"b_picked{t}")
             group_slots(turn_slots(picked), b_grouped[:, t * N : (t + 1) * N])
             if t < 2:
                 nc.scalar.copy(be_grouped[:, :, t], picked[:])
             else:
                 nc.vector.tensor_copy(be_grouped[:, :, t], picked[:])
+        bi_codes = sbuf([P, E], U32, "bi_codes")
+        bi_scales = sbuf([P, E], U8, "bi_scales")
+        nc.vector.quantize_mx(out=bi_codes[:].bitcast(E4M3), scales=bi_scales[:], in_=b_grouped[:, : N * PACK])
 
-        a_picked = [gather(a_win[k], f"a_picked{k}") for k in range(PACK)]
-
-        b_codes = sbuf([P, E + N], U32, "b_codes", "a_win0")
-        b_scales = sbuf([P, E + N], U8, "b_scales")
-        nc.vector.quantize_mx(out=b_codes[:].bitcast(E4M3), scales=b_scales[:], in_=b_grouped[:])
-
-        after_a1 = sbuf([P, N], BF16, "after_a1", "a_win1")
-        after_a2 = sbuf([P, 5 * N], F32, "after_a2", "a_win2")
-        after_a3 = sbuf([P, 2 * N], F32, "after_a3", "a_win3")
-        a_grouped = [
-            after_a3[:, N // 2 : N].bitcast(BF16) if k == 2 else sbuf([P, N], BF16, f"a_grouped{k}")[:]
-            for k in range(PACK)
-        ]
-        m_grouped = [after_a1[:], after_a3[:, : N // 2].bitcast(BF16)]
-        m_grouped += [sbuf([P, N], BF16, f"m_grouped{k}")[:] for k in (2, 3)]
-        scaled = [after_a2[:, :N] if k == 1 else sbuf([P, E], F32, f"scaled{k}")[:] for k in range(PACK)]
-        weight = [
-            sbuf([P, E], F32, "weight0")[:],
-            after_a2[:, 2 * N : 3 * N],
-            sbuf([P, E], F32, "weight2")[:],
-            after_a3[:, N:],
-        ]
-
-        def correlate(k):
-            group_slots(turn_slots(a_picked[k]), a_grouped[k])
-            a_codes = sbuf([P, P], U32, f"a_codes{k}")
-            a_scales = sbuf([P, P], U8, f"a_scales{k}")
-            nc.vector.quantize_mx(out=a_codes[:].bitcast(E4M3), scales=a_scales[:], in_=a_grouped[k])
+        def correlate(k, codes):
+            a_codes, a_scales = codes
             corr = psum2.tile([P, E], F32, name="corr")
             nc.tensor.matmul_mx(
                 out=corr[:],
                 lhsT=a_codes[:].bitcast(E4M3),
                 lhsT_scale=a_scales[:],
-                rhs=b_codes[:, :E].bitcast(E4M3),
-                rhs_scale=b_scales[:, :E],
+                rhs=bi_codes[:].bitcast(E4M3),
+                rhs_scale=bi_scales[:],
                 start=True,
                 stop=True,
             )
-            ca_k = ca_col[:, lanes[k] : lanes[k] + 1]
-            nc.vector.scalar_tensor_tensor(scaled[k], corr[:], ca_k, neg_cb_row[:], MULT, MULT)
+            return corr
 
-        def deal(k, dealt):
+        def scale_corr(k, corr, scaled):
             ca_k = ca_col[:, lanes[k] : lanes[k] + 1]
+            nc.vector.scalar_tensor_tensor(scaled, corr[:], ca_k, neg_cb_row[:], MULT, MULT)
+            return scaled
+
+        def deal_wm(k, dealt):
             nc.scalar.activation(
-                dealt[:, :E].rearrange("p (t q) -> p q t", t=PACK),
+                dealt.rearrange("p (t q) -> p q t", t=PACK),
                 wm_sb[k][:].rearrange("p (q t) -> p q t", t=PACK),
                 COPY,
-                scale=ca_k,
-            )
-            nc.scalar.copy(
-                dealt[:, E:].rearrange("p (t q) -> p q t", t=PACK), tg_sb[k][:].rearrange("p (q t) -> p q t", t=PACK)
+                scale=ca_col[:, lanes[k] : lanes[k] + 1],
             )
             return dealt
 
-        def make_weight(k, dealt):
-            w_bank = psum1.tile([P, PACK, P], F32, name="w_bank", tag="w_bank")
+        def deal_tg(k, dealt):
+            nc.scalar.copy(
+                dealt.rearrange("p (t q) -> p q t", t=PACK), tg_sb[k][:].rearrange("p (q t) -> p q t", t=PACK)
+            )
+            return dealt
+
+        def make_weight(dealt, weight, pool, tag):
+            w_bank = pool.tile([P, PACK, P], F32, name="w_bank", tag=tag)
             for t in range(PACK):
                 nc.tensor.transpose(w_bank[:, t, :], dealt[:, t * P : (t + 1) * P], ident[:])
             for t in range(PACK):
                 nc.scalar.activation(
-                    weight[k][:, t * P : (t + 1) * P], w_bank[:, t, :], COPY, scale=neg_cb_col[:, t : t + 1]
+                    weight[:, t * P : (t + 1) * P], w_bank[:, t, :], COPY, scale=neg_cb_col[:, t : t + 1]
                 )
+            return weight
 
-        def make_m(k, dealt):
+        def make_m(k, dealt, scaled, weight, m_grouped):
             resid = psum2.tile([P, PACK, P], F32, name="resid")
             for t in range(PACK):
                 nc.tensor.matmul(
                     resid[:, t, :],
-                    dealt[:, E + t * P : E + (t + 1) * P],
+                    dealt[:, t * P : (t + 1) * P],
                     ident[:],
                     is_transpose=True,
                     start=(t == 0),
@@ -184,95 +180,123 @@ def tile_attend_gbarlow_a_pl_kernel(tc, aT, bT, tg, wm, ca, cb, offs, out_0, out
             for t in range(PACK):
                 nc.tensor.matmul(
                     resid[:, t, :],
-                    scaled[k][:, t * P : (t + 1) * P],
+                    scaled[:, t * P : (t + 1) * P],
                     ident[:],
                     is_transpose=True,
                     start=False,
                     stop=(t == PACK - 1),
                 )
             nc.vector.tensor_tensor(
-                m_grouped[k].rearrange("p (c i t) -> p c t i", i=4, t=PACK),
+                m_grouped.rearrange("p (c i t) -> p c t i", i=4, t=PACK),
                 resid[:].rearrange("p t (c i) -> p c t i", i=4),
-                weight[k].rearrange("p (t c i) -> p c t i", i=4, t=PACK),
+                weight.rearrange("p (t c i) -> p c t i", i=4, t=PACK),
                 MULT,
             )
             m_codes = sbuf([P, P], U32, f"m_codes{k}")
             m_scales = sbuf([P, P], U8, f"m_scales{k}")
-            nc.vector.quantize_mx(out=m_codes[:].bitcast(E5M2), scales=m_scales[:], in_=m_grouped[k])
+            nc.vector.quantize_mx(out=m_codes[:].bitcast(E5M2), scales=m_scales[:], in_=m_grouped)
             return m_codes, m_scales
 
-        def place_gradient(k, m_codes, m_scales):
-            if k == 2:
-                grad = psum2.tile([P, N], F32, name="grad2", tag="turned")
-            else:
-                grad = psum1.tile([P, N], F32, name=f"grad{k}", tag="w_bank" if k == 3 else "grad")
+        def gradient(m, grad):
             nc.tensor.matmul_mx(
                 out=grad[:],
-                lhsT=m_codes[:].bitcast(E5M2),
-                lhsT_scale=m_scales[:],
-                rhs=b_codes[:, E:].bitcast(E4M3),
-                rhs_scale=b_scales[:, E:],
+                lhsT=m[0][:].bitcast(E5M2),
+                lhsT_scale=m[1][:],
+                rhs=be_codes[:].bitcast(E4M3),
+                rhs_scale=be_scales[:],
                 start=True,
                 stop=True,
             )
-            if k == 0:
-                grad_sb = after_a2[:, N : 2 * N]
-            else:
-                grad_sb = sbuf([P, N], F32, f"grad_sb{k}", "scaled3" if k == 1 else None)[:]
-            nc.scalar.copy(grad_sb, grad[:])
-            nc.vector.tensor_copy(out_win[k][:].indirect(offsets[:]), grad_sb)
+            return grad
+
+        def place(k, grad, parts):
+            width = N // len(parts)
+            for h, grad_sb in enumerate(parts):
+                nc.scalar.copy(grad_sb, grad[:, h * width : (h + 1) * width])
+                slots = offsets[:, h * width // 16 : (h + 1) * width // 16]
+                nc.vector.tensor_copy(out_win[k][:].indirect(slots), grad_sb)
             nc.sync.dma_start(out_rows[lanes[k]], out_win[k][:])
 
-        correlate(0)
-        dealt0 = deal(0, sbuf([P, 2 * E], F32, "dealt0", "a_picked0")[:])
-        make_weight(0, dealt0)
-        m0 = make_m(0, dealt0)
-        correlate(1)
-        dealt1 = deal(1, sbuf([P, 2 * E], F32, "dealt1", "a_picked1")[:])
-        place_gradient(0, *m0)
-        make_weight(1, dealt1)
-        dealt2 = deal(2, after_a2[:, 3 * N :])
-        make_weight(2, dealt2)
-        dealt3 = deal(3, sbuf([P, 2 * E], F32, "dealt3", "tg_sb2")[:])
-        m1 = make_m(1, dealt1)
-        correlate(2)
-        correlate(3)
-        make_weight(3, dealt3)
-        m2 = make_m(2, dealt2)
-        m3 = make_m(3, dealt3)
-        place_gradient(1, *m1)
-        place_gradient(2, *m2)
-        place_gradient(3, *m3)
+        def fresh(name, reuses=None):
+            return sbuf([P, E], F32, name, reuses)[:]
 
+        wm0 = deal_wm(0, fresh("wm_dealt0"))
+        tg0 = deal_tg(0, fresh("tg_dealt0"))
+        corr0 = correlate(0, codes0)
+        weight0 = make_weight(wm0, fresh("weight0"), psum1, "w_bank")
+        picked1 = gather(a_win[1], "a_picked1")
+        scaled0 = scale_corr(0, corr0, fresh("scaled0", "a_win1"))
+        codes1 = quantize_a(1, picked1, sbuf([P, N], BF16, "a_grouped1")[:])
+        be_codes = sbuf([P, N], U32, "be_codes", "a_picked1")
+        be_scales = sbuf([P, N], U8, "be_scales")
+        nc.vector.quantize_mx(out=be_codes[:].bitcast(E4M3), scales=be_scales[:], in_=b_grouped[:, N * PACK :])
+        corr1 = correlate(1, codes1)
+        m0 = make_m(0, tg0, scaled0, weight0, sbuf([P, N], BF16, "m_grouped0")[:])
+        wm1 = deal_wm(1, fresh("wm_dealt1"))
+        tg1 = deal_tg(1, fresh("tg_dealt1", "a_grouped1"))
+        scaled1 = scale_corr(1, corr1, fresh("scaled1"))
+        weight1 = make_weight(wm1, fresh("weight1"), psum1, "w_bank")
+        grad0 = gradient(m0, psum1.tile([P, N], F32, name="grad0", tag="grad"))
+
+        picked2 = gather(a_win[2], "a_picked2")
+        picked3 = gather(a_win[3], "a_picked3")
+        m1 = make_m(1, tg1, scaled1, weight1, sbuf([P, N], BF16, "m_grouped1", "a_win3")[:])
+        late = sbuf([P, 9 * N // 2], F32, "late", "tg_sb2")
+        codes2 = quantize_a(2, picked2, late[:, : N // 2].bitcast(BF16))
+        codes3 = quantize_a(3, picked3, late[:, N // 2 : N].bitcast(BF16))
+        corr2 = correlate(2, codes2)
+        corr3 = correlate(3, codes3)
+        grad1 = gradient(m1, psum2.tile([P, N], F32, name="grad1", tag="turned"))
+        scaled2 = scale_corr(2, corr2, fresh("scaled2"))
+        place(0, grad0, [late[:, N : 3 * N // 2], sbuf([P, N // 2], F32, "grad_sb0", "a_codes3")[:]])
+        scaled3 = scale_corr(3, corr3, fresh("scaled3"))
+        wm2 = deal_wm(2, fresh("wm_dealt2"))
+        tg2 = deal_tg(2, fresh("tg_dealt2"))
+        tg3 = deal_tg(3, late[:, 7 * N // 2 :])
+        wm3 = deal_wm(3, late[:, 5 * N // 2 : 7 * N // 2])
+        weight2 = make_weight(wm2, late[:, 3 * N // 2 : 5 * N // 2], psum1, "w_bank")
+        weight3 = make_weight(wm3, fresh("weight3"), psum2, "turned")
+        m2 = make_m(2, tg2, scaled2, weight2, sbuf([P, N], BF16, "m_grouped2")[:])
+        m3 = make_m(3, tg3, scaled3, weight3, sbuf([P, N], BF16, "m_grouped3")[:])
+        grads_sb = sbuf([P, 2 * N], F32, "grads_sb", "weight3")
+        place(1, grad1, [grads_sb[:, :N]])
+        grad2 = gradient(m2, psum1.tile([P, N], F32, name="grad2", tag="grad"))
+        place(2, grad2, [grads_sb[:, N:]])
+        grad3 = gradient(m3, psum1.tile([P, N], F32, name="grad3", tag="w_bank"))
+
+        spans = [(0, 1024), (1024, 1536), (1536, 2048)]
         pairs = [
-            sbuf([P, 2, HALF, 2], BF16, "pairs0", "a_picked3"),
-            sbuf([P, 2, HALF, 2], BF16, "pairs1", "a_grouped3"),
+            sbuf([P, 2, hi - lo, 2], BF16, f"pairs{n}", reuses)
+            for n, ((lo, hi), reuses) in enumerate(zip(spans, ("m_grouped3", "tg_sb2", "m_codes3")))
         ]
 
-        def round_plane(engine_copy, k, half):
-            lane = lanes[k]
-            engine_copy(pairs[half][:, lane // 2, :, lane % 2], out_win[k][:, half * HALF : (half + 1) * HALF])
+        def round_lane(engine_copy, k, n):
+            lo, hi = spans[n]
+            engine_copy(pairs[n][:, lanes[k] // 2, :, lanes[k] % 2], out_win[k][:, lo:hi])
 
         for k in range(PACK - 1):
-            for half in range(2):
-                round_plane(nc.scalar.copy, k, half)
+            for n in range(len(spans)):
+                round_lane(nc.scalar.copy, k, n)
+            if k == 0:
+                place(3, grad3, [fresh("grad_sb3", "out_win0")])
 
         plane_scales = sbuf([P, T], U8, "plane_scales")
-        copies = [nc.vector.tensor_copy, nc.scalar.copy]
-        laid = [sbuf([P, CHUNK * PACK], BF16, f"laid{c}") for c in range(T // CHUNK)]
-        for half in range(2):
-            round_plane(copies[half], PACK - 1, half)
-            words = pairs[half][:].rearrange("p u q h -> p u (q h)").bitcast(F32)
-            for part in range(2):
-                copies[half](
-                    laid[2 * half + part][:].bitcast(F32).rearrange("p (q u) -> p q u", u=2),
-                    words[:, :, part * CHUNK : (part + 1) * CHUNK].rearrange("p u q -> p q u"),
+        laid = []
+        for n, cuts in enumerate(((0, 512, 1024), (1024, 1536), (1536, 1792, 2048))):
+            engine_copy = nc.vector.tensor_copy if n == 0 else nc.scalar.copy
+            round_lane(engine_copy, PACK - 1, n)
+            words = pairs[n][:].rearrange("p u q h -> p u (q h)").bitcast(F32)
+            for lo, hi in zip(cuts, cuts[1:]):
+                tile = sbuf([P, (hi - lo) * PACK], BF16, f"laid{lo}")
+                engine_copy(
+                    tile[:].bitcast(F32).rearrange("p (q u) -> p q u", u=2),
+                    words[:, :, lo - cuts[0] : hi - cuts[0]].rearrange("p u q -> p q u"),
                 )
-        for c in range(T // CHUNK):
-            cols = slice(c * CHUNK, (c + 1) * CHUNK)
-            plane_codes = sbuf([P, CHUNK], U32, f"plane_codes{c}")
-            nc.vector.quantize_mx(out=plane_codes[:].bitcast(E4M3), scales=plane_scales[:, cols], in_=laid[c][:])
-            nc.sync.dma_start(out_words[:, cols], plane_codes[:].bitcast(I32))
+                laid.append((lo, hi, tile))
+        for lo, hi, tile in laid:
+            plane_codes = sbuf([P, hi - lo], U32, f"plane_codes{lo}")
+            nc.vector.quantize_mx(out=plane_codes[:].bitcast(E4M3), scales=plane_scales[:, lo:hi], in_=tile[:])
+            nc.sync.dma_start(out_words[:, lo:hi], plane_codes[:].bitcast(I32))
         for q in range(4):
             queue = nc.sync if q % 2 == 0 else nc.scalar
             queue.dma_start(out_scales[4 * q : 4 * q + 4, :], plane_scales[32 * q : 32 * q + 4, :].bitcast(I32))

@@ -231,14 +231,15 @@ def tile_attend_gbarlow_a_pl_kernel(tc, aT, bT, tg, wm, ca, cb, offs, out_0, out
         be_scales = sbuf([P, N], U8, "be_scales")
         nc.vector.quantize_mx(out=be_codes[:].bitcast(E4M3), scales=be_scales[:], in_=b_grouped[:, N * PACK :])
         corr1 = correlate(1, codes1)
-        m0 = make_m(0, tg0, scaled0, weight0, sbuf([P, N], BF16, "m_grouped0")[:])
+        picked2 = gather(a_win[2], "a_picked2")
+        after_a2 = sbuf([P, 3 * N // 2], F32, "after_a2", "a_win2")
+        m0 = make_m(0, tg0, scaled0, weight0, after_a2[:, : N // 2].bitcast(BF16))
         wm1 = deal_wm(1, fresh("wm_dealt1"))
         tg1 = deal_tg(1, fresh("tg_dealt1", "a_grouped1"))
-        scaled1 = scale_corr(1, corr1, fresh("scaled1"))
+        scaled1 = scale_corr(1, corr1, after_a2[:, N // 2 :])
         weight1 = make_weight(wm1, fresh("weight1"), psum1, "w_bank")
         grad0 = gradient(m0, psum1.tile([P, N], F32, name="grad0", tag="grad"))
 
-        picked2 = gather(a_win[2], "a_picked2")
         picked3 = gather(a_win[3], "a_picked3")
         m1 = make_m(1, tg1, scaled1, weight1, sbuf([P, N], BF16, "m_grouped1", "a_win3")[:])
         late = sbuf([P, 9 * N // 2], F32, "late", "tg_sb2")
@@ -258,7 +259,7 @@ def tile_attend_gbarlow_a_pl_kernel(tc, aT, bT, tg, wm, ca, cb, offs, out_0, out
         weight3 = make_weight(wm3, fresh("weight3"), psum2, "turned")
         m2 = make_m(2, tg2, scaled2, weight2, sbuf([P, N], BF16, "m_grouped2")[:])
         m3 = make_m(3, tg3, scaled3, weight3, sbuf([P, N], BF16, "m_grouped3")[:])
-        grads_sb = sbuf([P, 2 * N], F32, "grads_sb", "weight3")
+        grads_sb = sbuf([P, 2 * N], F32, "grads_sb", "scaled3")
         place(1, grad1, [grads_sb[:, :N]])
         grad2 = gradient(m2, psum1.tile([P, N], F32, name="grad2", tag="grad"))
         place(2, grad2, [grads_sb[:, N:]])
@@ -267,7 +268,7 @@ def tile_attend_gbarlow_a_pl_kernel(tc, aT, bT, tg, wm, ca, cb, offs, out_0, out
         spans = [(0, 1024), (1024, 1536), (1536, 2048)]
         pairs = [
             sbuf([P, 2, hi - lo, 2], BF16, f"pairs{n}", reuses)
-            for n, ((lo, hi), reuses) in enumerate(zip(spans, ("m_grouped3", "tg_sb2", "m_codes3")))
+            for n, ((lo, hi), reuses) in enumerate(zip(spans, ("m_grouped2", "tg_sb2", "weight3")))
         ]
 
         def round_lane(engine_copy, k, n):

@@ -78,7 +78,7 @@ def tile_attend_gbarlow_a_pl_kernel(tc, aT, bT, tg, wm, ca, cb, offs, out_0, out
 
         def zeroed_window(k):
             window = sbuf([P, T], F32, f"out_win{k}")
-            (nc.vector if k < 2 else nc.gpsimd).memset(window[:], 0.0)
+            nc.vector.memset(window[:].bitcast(I32), 0)
             return window
 
         def gather(window, name, reuses=None):

from contextlib import ExitStack

import concourse.mybir as mybir
from concourse.masks import make_identity

D, E, N, T = 512, 512, 512, 2048
FLOPS = 2 * 2 * D * E * N

F32 = mybir.dt.float32
BF16 = mybir.dt.bfloat16
I32 = mybir.dt.int32
U32 = mybir.dt.uint32
U16 = mybir.dt.uint16
U8 = mybir.dt.uint8
E4M3 = mybir.dt.float8_e4m3fn_x4
E5M2 = mybir.dt.float8_e5m2_x4
MULT = mybir.AluOpType.mult
COPY = mybir.ActivationFunctionType.Copy

P = 128
PACK = 4
CHUNK = 512
HALF = T // 2
ALIGN = 64


def tile_attend_gbarlow_a_pl_kernel(tc, aT, bT, tg, wm, ca, cb, offs, out_0, out_1, out_2):
    nc = tc.nc
    lanes = [(k + 1) % PACK for k in range(PACK)]
    a_rows = aT.rearrange("(p j) c -> j p c", j=PACK)
    b_rows = bT.rearrange("(p t) c -> t p c", t=PACK)
    tg_rows = tg.rearrange("(p j) e -> j p e", j=PACK)
    wm_rows = wm.rearrange("(p j) e -> j p e", j=PACK)
    out_rows = out_0.rearrange("(p j) c -> j p c", j=PACK)
    out_words = out_1[0].rearrange("p c l -> p (c l)").bitcast(I32)
    out_scales = out_2[0].bitcast(I32)

    with ExitStack() as ctx:
        keep = ctx.enter_context(tc.tile_pool(name="keep", bufs=1))
        psum1 = ctx.enter_context(tc.psum_pool(name="psum1", bufs=1))
        psum2 = ctx.enter_context(tc.psum_pool(name="psum2", bufs=2))

        def sbuf(shape, dtype, name, reuses=None):
            return keep.tile(shape, dtype, name=name, tag=reuses or name, align_bytes=ALIGN)

        offsets = keep.tile([P, N // 16], U16, name="offsets")
        nc.sync.dma_start(offsets[:], offs)
        cb_col = sbuf([P, PACK], F32, "cb_col")
        nc.scalar.dma_start(cb_col[:], cb[0].rearrange("(p t) -> p t", t=PACK))
        ca_col = sbuf([P, PACK], F32, "ca_col")
        nc.scalar.dma_start(ca_col[:], ca.rearrange("(p j) o -> p (j o)", j=PACK))

        b_win = [sbuf([P, T], F32, f"b_win{t}") for t in range(PACK)]
        a_win = [sbuf([P, T], F32, f"a_win{k}") for k in range(PACK)]
        tg_sb = [sbuf([P, E], F32, f"tg_sb{k}") for k in range(PACK)]
        wm_sb = [sbuf([P, E], F32, f"wm_sb{k}") for k in range(PACK)]
        for t in range(PACK - 1):
            nc.sync.dma_start(b_win[t][:], b_rows[t])
        nc.sync.dma_start(a_win[0][:], a_rows[lanes[0]])
        nc.sync.dma_start(b_win[PACK - 1][:], b_rows[PACK - 1])
        for windows, weighted in (((), (0,)), ((1,), (1,)), ((2, 3), (2, 3))):
            for k in windows:
                nc.sync.dma_start(a_win[k][:], a_rows[lanes[k]])
            for k in weighted:
                nc.sync.dma_start(wm_sb[k][:], wm_rows[lanes[k]])
                nc.sync.dma_start(tg_sb[k][:], tg_rows[lanes[k]])

        ident = sbuf([P, P], F32, "ident")
        make_identity(nc, ident[:])

        neg_cb_col = sbuf([P, PACK], F32, "neg_cb_col")
        nc.scalar.activation(neg_cb_col[:], cb_col[:], COPY, scale=-1.0)
        spread = psum1.tile([P, PACK, P], F32, name="spread", tag="w_bank")
        for t in range(PACK):
            nc.tensor.transpose(spread[:, t, :], neg_cb_col[:, t : t + 1].to_broadcast([P, P]), ident[:])
        neg_cb_row = sbuf([P, E], F32, "neg_cb_row")
        nc.scalar.copy(neg_cb_row[:], spread[:].rearrange("p t q -> p (t q)"))

        def zeroed_window(k):
            window = sbuf([P, T], F32, f"out_win{k}")
            nc.vector.memset(window[:].bitcast(I32), 0)
            return window

        def gather(window, name, reuses=None):
            picked = sbuf([P, N], BF16, name, reuses)
            nc.vector.tensor_copy(picked[:], window[:].indirect(offsets[:]))
            return picked

        def turn_slots(picked):
            words = picked[:].bitcast(F32)
            turned = psum2.tile([P, 2, P], F32, name="turned")
            for u in range(2):
                nc.tensor.transpose(turned[:, u, :], words[:, u : N // 2 : 2], ident[:])
            return turned

        def group_slots(turned, grouped):
            nc.scalar.copy(
                grouped.bitcast(F32).rearrange("p (q u) -> p q u", u=2), turned[:].rearrange("p u q -> p q u")
            )

        out_win = [zeroed_window(k) for k in range(PACK)]
        b_grouped = sbuf([P, 2 * N * PACK], BF16, "b_grouped")
        be_grouped = b_grouped[:, N * PACK :].rearrange("p (i t) -> p i t", t=PACK)

        def quantize_a(k, picked, grouped, reuses=None):
            group_slots(turn_slots(picked), grouped)
            a_codes = sbuf([P, P], U32, f"a_codes{k}", reuses)
            a_scales = sbuf([P, P], U8, f"a_scales{k}")
            nc.vector.quantize_mx(out=a_codes[:].bitcast(E4M3), scales=a_scales[:], in_=grouped)
            return a_codes, a_scales

        for t in range(PACK):
            if t == PACK - 1:
                codes0 = quantize_a(0, gather(a_win[0], "a_picked0"), sbuf([P, N], BF16, "a_grouped0")[:], "b_win3")
            picked = gather(b_win[t], f"b_picked{t}")
            group_slots(turn_slots(picked), b_grouped[:, t * N : (t + 1) * N])
            if t < 2:
                nc.scalar.copy(be_grouped[:, :, t], picked[:])
            else:
                nc.vector.tensor_copy(be_grouped[:, :, t], picked[:])
        bi_codes = sbuf([P, E], U32, "bi_codes")
        bi_scales = sbuf([P, E], U8, "bi_scales")
        nc.vector.quantize_mx(out=bi_codes[:].bitcast(E4M3), scales=bi_scales[:], in_=b_grouped[:, : N * PACK])

        def correlate(k, codes):
            a_codes, a_scales = codes
            corr = psum2.tile([P, E], F32, name="corr")
            nc.tensor.matmul_mx(
                out=corr[:],
                lhsT=a_codes[:].bitcast(E4M3),
                lhsT_scale=a_scales[:],
                rhs=bi_codes[:].bitcast(E4M3),
                rhs_scale=bi_scales[:],
                start=True,
                stop=True,
            )
            return corr

        def scale_corr(k, corr, scaled):
            ca_k = ca_col[:, lanes[k] : lanes[k] + 1]
            nc.vector.scalar_tensor_tensor(scaled, corr[:], ca_k, neg_cb_row[:], MULT, MULT)
            return scaled

        def deal_wm(k, dealt):
            nc.scalar.activation(
                dealt.rearrange("p (t q) -> p q t", t=PACK),
                wm_sb[k][:].rearrange("p (q t) -> p q t", t=PACK),
                COPY,
                scale=ca_col[:, lanes[k] : lanes[k] + 1],
            )
            return dealt

        def deal_tg(k, dealt):
            nc.scalar.copy(
                dealt.rearrange("p (t q) -> p q t", t=PACK), tg_sb[k][:].rearrange("p (q t) -> p q t", t=PACK)
            )
            return dealt

        def make_weight(dealt, weight, pool, tag):
            w_bank = pool.tile([P, PACK, P], F32, name="w_bank", tag=tag)
            for t in range(PACK):
                nc.tensor.transpose(w_bank[:, t, :], dealt[:, t * P : (t + 1) * P], ident[:])
            for t in range(PACK):
                nc.scalar.activation(
                    weight[:, t * P : (t + 1) * P], w_bank[:, t, :], COPY, scale=neg_cb_col[:, t : t + 1]
                )
            return weight

        def make_m(k, dealt, scaled, weight, m_grouped):
            resid = psum2.tile([P, PACK, P], F32, name="resid")
            for t in range(PACK):
                nc.tensor.matmul(
                    resid[:, t, :],
                    dealt[:, t * P : (t + 1) * P],
                    ident[:],
                    is_transpose=True,
                    start=(t == 0),
                    stop=False,
                )
            for t in range(PACK):
                nc.tensor.matmul(
                    resid[:, t, :],
                    scaled[:, t * P : (t + 1) * P],
                    ident[:],
                    is_transpose=True,
                    start=False,
                    stop=(t == PACK - 1),
                )
            nc.vector.tensor_tensor(
                m_grouped.rearrange("p (c i t) -> p c t i", i=4, t=PACK),
                resid[:].rearrange("p t (c i) -> p c t i", i=4),
                weight.rearrange("p (t c i) -> p c t i", i=4, t=PACK),
                MULT,
            )
            m_codes = sbuf([P, P], U32, f"m_codes{k}")
            m_scales = sbuf([P, P], U8, f"m_scales{k}")
            nc.vector.quantize_mx(out=m_codes[:].bitcast(E5M2), scales=m_scales[:], in_=m_grouped)
            return m_codes, m_scales

        def gradient(m, grad):
            nc.tensor.matmul_mx(
                out=grad[:],
                lhsT=m[0][:].bitcast(E5M2),
                lhsT_scale=m[1][:],
                rhs=be_codes[:].bitcast(E4M3),
                rhs_scale=be_scales[:],
                start=True,
                stop=True,
            )
            return grad

        def place(k, grad, parts):
            width = N // len(parts)
            for h, grad_sb in enumerate(parts):
                nc.scalar.copy(grad_sb, grad[:, h * width : (h + 1) * width])
                slots = offsets[:, h * width // 16 : (h + 1) * width // 16]
                nc.vector.tensor_copy(out_win[k][:].indirect(slots), grad_sb)
            nc.sync.dma_start(out_rows[lanes[k]], out_win[k][:])

        def fresh(name, reuses=None):
            return sbuf([P, E], F32, name, reuses)[:]

        wm0 = deal_wm(0, fresh("wm_dealt0"))
        tg0 = deal_tg(0, fresh("tg_dealt0"))
        corr0 = correlate(0, codes0)
        weight0 = make_weight(wm0, fresh("weight0"), psum1, "w_bank")
        picked1 = gather(a_win[1], "a_picked1")
        scaled0 = scale_corr(0, corr0, fresh("scaled0", "a_win1"))
        codes1 = quantize_a(1, picked1, sbuf([P, N], BF16, "a_grouped1")[:])
        be_codes = sbuf([P, N], U32, "be_codes", "a_picked1")
        be_scales = sbuf([P, N], U8, "be_scales")
        nc.vector.quantize_mx(out=be_codes[:].bitcast(E4M3), scales=be_scales[:], in_=b_grouped[:, N * PACK :])
        corr1 = correlate(1, codes1)
        picked2 = gather(a_win[2], "a_picked2")
        after_a2 = sbuf([P, 3 * N // 2], F32, "after_a2", "a_win2")
        m0 = make_m(0, tg0, scaled0, weight0, after_a2[:, : N // 2].bitcast(BF16))
        wm1 = deal_wm(1, fresh("wm_dealt1"))
        tg1 = deal_tg(1, fresh("tg_dealt1", "a_grouped1"))
        scaled1 = scale_corr(1, corr1, after_a2[:, N // 2 :])
        weight1 = make_weight(wm1, fresh("weight1"), psum1, "w_bank")
        grad0 = gradient(m0, psum1.tile([P, N], F32, name="grad0", tag="grad"))

        picked3 = gather(a_win[3], "a_picked3")
        m1 = make_m(1, tg1, scaled1, weight1, sbuf([P, N], BF16, "m_grouped1", "a_win3")[:])
        late = sbuf([P, 9 * N // 2], F32, "late", "tg_sb2")
        codes2 = quantize_a(2, picked2, late[:, : N // 2].bitcast(BF16))
        codes3 = quantize_a(3, picked3, late[:, N // 2 : N].bitcast(BF16))
        corr2 = correlate(2, codes2)
        corr3 = correlate(3, codes3)
        grad1 = gradient(m1, psum2.tile([P, N], F32, name="grad1", tag="turned"))
        scaled2 = scale_corr(2, corr2, fresh("scaled2"))
        place(0, grad0, [late[:, N : 3 * N // 2], sbuf([P, N // 2], F32, "grad_sb0", "a_codes3")[:]])
        scaled3 = scale_corr(3, corr3, fresh("scaled3"))
        wm2 = deal_wm(2, fresh("wm_dealt2"))
        tg2 = deal_tg(2, fresh("tg_dealt2"))
        tg3 = deal_tg(3, late[:, 7 * N // 2 :])
        wm3 = deal_wm(3, late[:, 5 * N // 2 : 7 * N // 2])
        weight2 = make_weight(wm2, late[:, 3 * N // 2 : 5 * N // 2], psum1, "w_bank")
        weight3 = make_weight(wm3, fresh("weight3"), psum2, "turned")
        m2 = make_m(2, tg2, scaled2, weight2, sbuf([P, N], BF16, "m_grouped2")[:])
        m3 = make_m(3, tg3, scaled3, weight3, sbuf([P, N], BF16, "m_grouped3")[:])
        grads_sb = sbuf([P, 2 * N], F32, "grads_sb", "scaled3")
        place(1, grad1, [grads_sb[:, :N]])
        grad2 = gradient(m2, psum1.tile([P, N], F32, name="grad2", tag="grad"))
        place(2, grad2, [grads_sb[:, N:]])
        grad3 = gradient(m3, psum1.tile([P, N], F32, name="grad3", tag="w_bank"))

        spans = [(0, 1024), (1024, 1536), (1536, 2048)]
        pairs = [
            sbuf([P, 2, hi - lo, 2], BF16, f"pairs{n}", reuses)
            for n, ((lo, hi), reuses) in enumerate(zip(spans, ("m_grouped2", "tg_sb2", "weight3")))
        ]

        def round_lane(engine_copy, k, n):
            lo, hi = spans[n]
            engine_copy(pairs[n][:, lanes[k] // 2, :, lanes[k] % 2], out_win[k][:, lo:hi])

        for k in range(PACK - 1):
            for n in range(len(spans)):
                round_lane(nc.scalar.copy, k, n)
            if k == 0:
                place(3, grad3, [fresh("grad_sb3", "out_win0")])

        plane_scales = sbuf([P, T], U8, "plane_scales")
        laid = []
        for n, cuts in enumerate(((0, 512, 1024), (1024, 1536), (1536, 1792, 2048))):
            engine_copy = nc.vector.tensor_copy if n == 0 else nc.scalar.copy
            round_lane(engine_copy, PACK - 1, n)
            words = pairs[n][:].rearrange("p u q h -> p u (q h)").bitcast(F32)
            for lo, hi in zip(cuts, cuts[1:]):
                tile = sbuf([P, (hi - lo) * PACK], BF16, f"laid{lo}")
                engine_copy(
                    tile[:].bitcast(F32).rearrange("p (q u) -> p q u", u=2),
                    words[:, :, lo - cuts[0] : hi - cuts[0]].rearrange("p u q -> p q u"),
                )
                laid.append((lo, hi, tile))
        for lo, hi, tile in laid:
            plane_codes = sbuf([P, hi - lo], U32, f"plane_codes{lo}")
            nc.vector.quantize_mx(out=plane_codes[:].bitcast(E4M3), scales=plane_scales[:, lo:hi], in_=tile[:])
            nc.sync.dma_start(out_words[:, lo:hi], plane_codes[:].bitcast(I32))
        for q in range(4):
            queue = nc.sync if q % 2 == 0 else nc.scalar
            queue.dma_start(out_scales[4 * q : 4 * q + 4, :], plane_scales[32 * q : 32 * q + 4, :].bitcast(I32))
